import numpy as np
import ml_dtypes


def mxq(x, axis, fmt="e4m3"):
    dtype, down = {"e4m3": (ml_dtypes.float8_e4m3fn, 7), "e5m2": (ml_dtypes.float8_e5m2, 14)}[fmt]
    v = np.moveaxis(np.asarray(x, np.float32).astype(ml_dtypes.bfloat16).astype(np.float64), axis, -1)
    blocks = v.reshape(v.shape[:-1] + (-1, 32))
    amax = np.abs(blocks).max(-1, keepdims=True)
    byte = np.maximum(np.where(amax > 0, np.frexp(amax)[1] - 1 + 127, 0) - down, 1)
    scale = np.exp2(byte - 127.0)
    codes = (blocks / scale).astype(np.float32).astype(dtype).astype(np.float64)
    return np.moveaxis((codes * scale).reshape(v.shape), -1, axis)


WIDE = False


def mx_kscale(k):
    if not WIDE:
        return np.ones(k)
    levels = np.array([10, -10, 5, -5, 0])
    if k % 512:
        return np.exp2(np.random.permutation(np.resize(levels, k // 32))).repeat(32)
    a = np.empty((k // 512, 16))
    for p in range(k // 512):
        a[p, :8] = np.random.permutation(np.resize(levels, 8))
        for g in range(8):
            far = levels[np.abs(levels - a[p, g]) >= 10]
            a[p, g + 8] = far[np.random.randint(len(far))]
    return np.exp2(a.ravel()).repeat(32)


def f64(x):
    return np.asarray(x).astype(np.float64)


def striped8(idx):
    return np.asarray(idx).reshape(8, -1, 16).transpose(0, 2, 1).reshape(128, -1).astype(np.uint16)


def unstriped8(offs):
    return offs.reshape(8, 16, -1).transpose(0, 2, 1).reshape(8, -1).astype(np.int64)


def pick8(x, idx, run):
    r = np.arange(len(x))
    return x[r[:, None], idx[r % (8 * run) // run]]


E2M1 = np.array([0.0, 0.5, 1.0, 1.5, 2.0, 3.0, 4.0, 6.0, -0.0, -0.5, -1.0, -1.5, -2.0, -3.0, -4.0, -6.0])


def pack_weight(w, fmt):
    k, n = w.shape
    w = f64(np.asarray(w, np.float32).astype(ml_dtypes.bfloat16)).reshape(k // 32, 32, n)
    amax = np.abs(w).max(1)
    if fmt == "e4m3":
        byte = np.frexp(amax)[1] - 1 + 127 - 7
    else:
        mant, ex = np.frexp(amax / 6.0)
        byte = np.where(mant > 0.5, ex, ex - 1) + 127
    byte = np.clip(np.where(amax > 0, byte, 1), 1, 254)
    scaled = (w * np.exp2(127.0 - byte)[:, None, :]).reshape(k, n).astype(np.float32)
    by_word = np.ascontiguousarray(scaled.reshape(k // 512, 128, 4, n).transpose(0, 1, 3, 2))
    if fmt == "e4m3":
        words = by_word.astype(ml_dtypes.float8_e4m3fn).view(np.uint8)
    else:
        c = by_word.astype(ml_dtypes.float4_e2m1fn).view(np.uint8) & 0xF
        words = (c[..., 0::2] | (c[..., 1::2] << 4)).reshape(k // 512, 128, 2 * n)
    return np.ascontiguousarray(words), np.ascontiguousarray(byte.astype(np.uint8).reshape(k // 512, 16, n))


def unpack_weight(words, scales, fmt):
    g, _, n = scales.shape
    words = np.ascontiguousarray(words).reshape(g, 128, n, -1)
    if fmt == "e4m3":
        vals = words.view(ml_dtypes.float8_e4m3fn).astype(np.float64)
    else:
        nib = np.empty((g, 128, n, 4), np.uint8)
        nib[..., 0::2] = words & 0xF
        nib[..., 1::2] = words >> 4
        vals = E2M1[nib]
    vals = vals * np.repeat(np.exp2(scales.astype(np.float64) - 127.0), 8, axis=1)[..., None]
    return vals.transpose(0, 1, 3, 2).reshape(g * 512, n)


D, T, U, I, J, Q, E = 512, 1024, 1024, 512, 256, 512, 256


def setup_inputs():
    n = np.random.standard_normal
    idx = np.stack([np.random.permutation(T)[:J] for _ in range(8)])
    idx2 = np.stack([np.random.permutation(U)[:J] for _ in range(8)])
    idx3 = np.stack([np.random.permutation(T)[:I] for _ in range(8)])
    idx4 = np.stack([np.random.permutation(T)[:I] for _ in range(8)])
    fd = mx_kscale(D)
    fq = mx_kscale(Q)
    keysp = pack_weight(n((D, T)) / fd[:, None], "e2m1")
    notesp = pack_weight(n((D, U)) / fd[:, None], "e4m3")
    mixp = pack_weight(n((Q, E)) * 1.0 / np.sqrt(Q) / fq[:, None], "e4m3")
    return {
        "query": (n((D, Q)) * 1.0 / np.sqrt(D) * fd[:, None]).astype(np.float32),
        "query2": (n((D, Q)) * 1.0 / np.sqrt(D) * fd[:, None]).astype(np.float32),
        "keys_words": keysp[0],
        "keys_scales": keysp[1],
        "notes_words": notesp[0],
        "notes_scales": notesp[1],
        "rowf": (np.random.uniform(0.5, 2.0, (Q, 1)) * fq[:, None]).astype(np.float32),
        "mix_words": mixp[0],
        "mix_scales": mixp[1],
        "offs": striped8(idx),
        "offs2": striped8(idx2),
        "offs3": striped8(idx3),
        "offs4": striped8(idx4),
    }


def reference(query, query2, keys_words, keys_scales, notes_words, notes_scales, rowf, mix_words, mix_scales, offs, offs2, offs3, offs4):
    idx = unstriped8(offs)
    idx2 = unstriped8(offs2)
    idx3 = unstriped8(offs3)
    idx4 = unstriped8(offs4)
    keysu = unpack_weight(keys_words, keys_scales, "e2m1")
    notesu = unpack_weight(notes_words, notes_scales, "e4m3")
    mixu = unpack_weight(mix_words, mix_scales, "e4m3")
    queryq = mxq(f64(query), 0, "e4m3")
    a = queryq.T @ keysu
    query2q = mxq(f64(query2), 0, "e4m3")
    b = query2q.T @ notesu
    w = np.concatenate([pick8(a, idx, 64), pick8(b, idx2, 64)], axis=1)
    f1 = np.zeros((Q, T))
    f1[np.arange(Q)[:, None], idx3[np.arange(Q) % 512 // 64]] = w
    cc = a - f1
    g = pick8(cc, idx4, 64) + w
    gw = g * f64(rowf)
    gwq = mxq(gw, 0, "e4m3")
    y = mixu.T @ gwq
    return y

@@ -1,0 +1,207 @@
+from contextlib import ExitStack
+
+import concourse.mybir as mybir
+
+D, T, U, I, J, Q, E = 512, 1024, 1024, 512, 256, 512, 256
+FLOPS = 2 * D * Q * T + 2 * D * Q * U + 2 * Q * E * I
+
+F32 = mybir.dt.float32
+BF16 = mybir.dt.bfloat16
+I32 = mybir.dt.int32
+U32 = mybir.dt.uint32
+U16 = mybir.dt.uint16
+U8 = mybir.dt.uint8
+FP8X4 = mybir.dt.float8_e4m3fn_x4
+FP4X4 = mybir.dt.float4_e2m1fn_x4
+ALU = mybir.AluOpType
+COPY = mybir.ActivationFunctionType.Copy
+
+P = 128
+PACK = 4
+BANK = 512
+
+
+def tile_attend_joinedput_twoq_mixed_kernel(tc, query, query2, keys_words, keys_scales, notes_words, notes_scales,
+                                             rowf, mix_words, mix_scales, offs, offs2, offs3, offs4, out):
+    nc = tc.nc
+    with ExitStack() as ctx:
+        keep = ctx.enter_context(tc.tile_pool(name="keep", bufs=1))
+        score_banks = ctx.enter_context(tc.psum_pool(name="score_banks", bufs=4))
+        out_banks = ctx.enter_context(tc.psum_pool(name="out_banks", bufs=4))
+
+        def load_list(name, src, n):
+            tile = keep.tile([P, n // 16], U16, name=name)
+            nc.sync.dma_start(tile[:], src)
+            return tile
+
+        def zeroed_plane(name, width):
+            tile = keep.tile([P, width], U8, name=name, align_bytes=64)
+            nc.vector.memset(tile[:].bitcast(I32), 0)
+            return tile
+
+        def load_plane(queue, tile, src):
+            for quad in range(4):
+                queue.dma_start(tile[32 * quad:32 * quad + 4, :].bitcast(I32), src[0, 4 * quad:4 * quad + 4, :].bitcast(I32))
+
+        def load_query_half(name, src, half):
+            tile = keep.tile([P, PACK, Q // 2], F32, name=name)
+            nc.sync.dma_start(tile[:], src.rearrange("(p j) q -> p j q", j=PACK)[:, :, half * (Q // 2):(half + 1) * (Q // 2)])
+            return tile
+
+        keys_plane = zeroed_plane("keys_plane", T)
+        notes_plane = zeroed_plane("notes_plane", U)
+        mix_plane = zeroed_plane("mix_plane", E)
+
+        q_raw = [load_query_half("q_raw%d" % h, query, h) for h in range(2)]
+        keys_w = keep.tile([P, 2 * T], U8, name="keys_w", align_bytes=64)
+        nc.sync.dma_start(keys_w[:].bitcast(I32), keys_words[0].bitcast(I32))
+        load_plane(nc.scalar, keys_plane, keys_scales)
+        list_a = load_list("list_a", offs, J)
+        q2_raw = [load_query_half("q2_raw%d" % h, query2, h) for h in range(2)]
+        notes_w = keep.tile([P, U], I32, name="notes_w", align_bytes=64)
+        nc.sync.dma_start(notes_w[:], notes_words[0].rearrange("p n t -> p (n t)").bitcast(I32))
+        list_put = load_list("list_put", offs3, I)
+        load_plane(nc.sync, notes_plane, notes_scales)
+        list_b = load_list("list_b", offs2, J)
+        list_cc = load_list("list_cc", offs4, I)
+        factors = keep.tile([P, PACK], F32, name="factors")
+        nc.sync.dma_start(factors[:], rowf.rearrange("(p t) o -> p (t o)", t=PACK))
+        mix_w = keep.tile([P, E], I32, name="mix_w", align_bytes=64)
+        nc.sync.dma_start(mix_w[:], mix_words[0].rearrange("p n t -> p (n t)").bitcast(I32))
+        load_plane(nc.sync, mix_plane, mix_scales)
+
+        placed = [keep.tile([P, T], F32, name="placed%d" % k) for k in range(3)]
+        for tile in placed:
+            nc.vector.memset(tile[:], 0.0)
+
+        def deal(copy, dealt, raw, half, t0, t1):
+            src = raw[half][:].rearrange("p j (m t) -> p m t j", t=PACK)[:, :, t0:t1]
+            dst = dealt[:].rearrange("p t m j -> p m t j")[:, 64 * half:64 * (half + 1), t0:t1]
+            copy(dst, src)
+
+        def quantize_rows(codes, plane, dealt, t0, t1):
+            nc.vector.quantize_mx(
+                out=codes[:, t0 * P:t1 * P].bitcast(FP8X4),
+                scales=plane[:, t0 * P:t1 * P],
+                in_=dealt[:, t0:t1].rearrange("p t m j -> p (t m j)"),
+            )
+
+        q_dealt = keep.tile([P, PACK, P, PACK], BF16, name="q_dealt", align_bytes=64)
+        q_codes = keep.tile([P, Q], U32, name="q_codes", align_bytes=64)
+        q_plane = keep.tile([P, Q], U8, name="q_plane", align_bytes=64)
+        q2_dealt = keep.tile([P, PACK, P, PACK], BF16, name="q2_dealt", align_bytes=64)
+        q2_codes = keep.tile([P, Q], U32, name="q2_codes", align_bytes=64)
+        q2_plane = keep.tile([P, Q], U8, name="q2_plane", align_bytes=64)
+
+        a = [keep.tile([P, T], F32, name="a%d" % t) for t in range(PACK)]
+        b = [keep.tile([P, U], F32, name="b%d" % t) for t in range(PACK)]
+        w = [keep.tile([P, I], F32, name="w%d" % t) for t in range(PACK)]
+        g = [keep.tile([P, I], F32, name="g%d" % t)[:] for t in (0, 1, 3)]
+        cc = [keep.tile([P, T], F32, name="cc%d" % t) for t in range(PACK)]
+        a_banks = {}
+
+        def scores(t, codes, plane, words, pool_plane):
+            banks = []
+            for n in range(2):
+                bank = score_banks.tile([P, BANK], F32, name="score_bank")
+                nc.tensor.matmul_mx(out=bank[:], lhsT=codes[:, t * P:(t + 1) * P].bitcast(FP8X4),
+                                    lhsT_scale=plane[:, t * P:(t + 1) * P], rhs=words(n),
+                                    rhs_scale=pool_plane[:, n * BANK:(n + 1) * BANK], start=True, stop=True)
+                banks.append(bank)
+            return banks
+
+        def keys_cols(n):
+            return keys_w[:, 2 * n * BANK:2 * (n + 1) * BANK].bitcast(FP4X4)
+
+        def notes_cols(n):
+            return notes_w[:, n * BANK:(n + 1) * BANK].bitcast(FP8X4)
+
+        def scalar_gather(dst, src):
+            nc.scalar.activation(dst, src, COPY)
+
+        def put(t, part):
+            nc.vector.tensor_copy(placed[t % 3][:].indirect(list_put[:, 16 * part:16 * (part + 1)]), w[t][:, part * J:(part + 1) * J])
+
+        def part_a(t, second_copy, gather):
+            banks = scores(t, q_codes, q_plane, keys_cols, keys_plane)
+            a_banks[t] = banks
+            nc.scalar.copy(a[t][:, :BANK], banks[0][:])
+            second_copy(a[t][:, BANK:], banks[1][:])
+            gather(w[t][:, :J], a[t][:].indirect(list_a[:]))
+            put(t, 0)
+
+        def part_b(t):
+            banks = scores(t, q2_codes, q2_plane, notes_cols, notes_plane)
+            nc.scalar.copy(b[t][:, :BANK], banks[0][:])
+            nc.scalar.copy(b[t][:, BANK:], banks[1][:])
+            scalar_gather(w[t][:, J:], b[t][:].indirect(list_b[:]))
+            put(t, 1)
+
+        def take_off(t):
+            nc.gpsimd.tensor_tensor(cc[t][:], a[t][:], placed[t % 3][:], ALU.subtract)
+
+        def gpsimd_cast(dst, src):
+            nc.gpsimd.tensor_scalar(dst, src, 1.0, 0.0, ALU.mult, ALU.add)
+
+        deal(nc.vector.tensor_copy, q_dealt, q_raw, 0, 0, 4)
+        deal(nc.vector.tensor_copy, q_dealt, q_raw, 1, 0, 1)
+        deal(nc.scalar.copy, q_dealt, q_raw, 1, 3, 4)
+        deal(nc.vector.tensor_copy, q_dealt, q_raw, 1, 1, 3)
+        quantize_rows(q_codes, q_plane, q_dealt, 0, 1)
+        quantize_rows(q_codes, q_plane, q_dealt, 1, 4)
+        part_a(0, nc.vector.tensor_copy, nc.vector.tensor_copy)
+        deal(nc.vector.tensor_copy, q2_dealt, q2_raw, 0, 0, 4)
+        deal(gpsimd_cast, q2_dealt, q2_raw, 1, 0, 1)
+        deal(gpsimd_cast, q2_dealt, q2_raw, 1, 1, 4)
+        quantize_rows(q2_codes, q2_plane, q2_dealt, 0, 1)
+        quantize_rows(q2_codes, q2_plane, q2_dealt, 1, 4)
+        part_a(1, nc.scalar.copy, scalar_gather)
+        part_b(0)
+        take_off(0)
+        part_a(2, nc.scalar.copy, scalar_gather)
+        last = PACK - 1
+        for t in range(1, last):
+            part_b(t)
+            take_off(t)
+        part_a(last, nc.scalar.copy, scalar_gather)
+        part_b(last)
+        for n in range(2):
+            cols = slice(n * BANK, (n + 1) * BANK)
+            nc.vector.tensor_tensor(cc[last][:, cols], a_banks[last][n][:], placed[last % 3][:, cols], ALU.subtract)
+
+        pair_tile = keep.tile([P, 2, I, 2], BF16, name="pair_tile", align_bytes=64)
+        gw = keep.tile([P, I, PACK], BF16, name="gw", align_bytes=64)
+        gw_codes = keep.tile([P, I], U32, name="gw_codes", align_bytes=64)
+        gw_plane = keep.tile([P, I], U8, name="gw_plane", align_bytes=64)
+
+        def scale(t, slots):
+            nc.scalar.activation(pair_tile[:, t // 2, slots, t % 2], g[t][:, slots], COPY, scale=factors[:, t:t + 1])
+
+        left = keep.tile([P, 3, I], F32, name="b%d" % last)
+        g.insert(2, left[:, 2, :])
+        for t in range(2):
+            scalar_gather(left[:, t, :], cc[t][:].indirect(list_cc[:]))
+        for t in range(2):
+            nc.vector.tensor_tensor(g[t], left[:, t, :], w[t][:], ALU.add)
+            scale(t, slice(0, I))
+        nc.vector.tensor_tensor(g[2], cc[2][:].indirect(list_cc[:]), w[2][:], ALU.add)
+        scale(2, slice(0, I))
+        for half in range(2):
+            slots = slice(half * J, (half + 1) * J)
+            nc.vector.tensor_tensor(g[last][:, slots], cc[last][:].indirect(list_cc[:, 16 * half:16 * (half + 1)]), w[last][:, slots], ALU.add)
+            scale(last, slots)
+        pair_words = pair_tile[:].rearrange("p k i r -> p k (i r)").bitcast(I32)
+        gw_words = gw[:].rearrange("p i t -> p (i t)").bitcast(I32).rearrange("p (i k) -> p i k", k=2)
+        for half in range(2):
+            slots = slice(half * J, (half + 1) * J)
+            nc.vector.tensor_copy(gw_words[:, slots, :], pair_words[:, :, slots].rearrange("p k i -> p i k"))
+            nc.vector.quantize_mx(out=gw_codes[:, slots].bitcast(FP8X4), scales=gw_plane[:, slots],
+                                  in_=gw[:, slots, :].rearrange("p i t -> p (i t)"))
+            for e, copy in enumerate((nc.scalar.copy, nc.vector.tensor_copy)):
+                chans = slice(e * P, (e + 1) * P)
+                bank = out_banks.tile([P, J], F32, name="out_bank")
+                nc.tensor.matmul_mx(out=bank[:], lhsT=mix_w[:, chans].bitcast(FP8X4), lhsT_scale=mix_plane[:, chans],
+                                    rhs=gw_codes[:, slots].bitcast(FP8X4), rhs_scale=gw_plane[:, slots], start=True, stop=True)
+                staged = keep.tile([P, J], F32, name="staged%d_%d" % (half, e))
+                copy(staged[:], bank[:])
+                nc.sync.dma_start(out[chans, slots], staged[:])

@@ -36,7 +36,7 @@ def tile_attend_joinedput_twoq_mixed_kernel(tc, query, query2, keys_words, keys_
 
         def zeroed_plane(name, width):
             tile = keep.tile([P, width], U8, name=name, align_bytes=64)
-            nc.vector.memset(tile[:].bitcast(I32), 0)
+            nc.gpsimd.memset(tile[:].bitcast(I32), 0)
             return tile
 
         def load_plane(queue, tile, src):
@@ -52,15 +52,17 @@ def tile_attend_joinedput_twoq_mixed_kernel(tc, query, query2, keys_words, keys_
         notes_plane = zeroed_plane("notes_plane", U)
         mix_plane = zeroed_plane("mix_plane", E)
 
-        q_raw = [load_query_half("q_raw%d" % h, query, h) for h in range(2)]
+        q_raw = [load_query_half("q_raw0", query, 0)]
+        keys_rows = keep.tile([P, T], U8, name="keys_rows", align_bytes=64)
+        load_plane(nc.sync, keys_rows, keys_scales)
+        q_raw.append(load_query_half("q_raw1", query, 1))
         keys_w = keep.tile([P, 2 * T], U8, name="keys_w", align_bytes=64)
         nc.sync.dma_start(keys_w[:].bitcast(I32), keys_words[0].bitcast(I32))
-        load_plane(nc.scalar, keys_plane, keys_scales)
-        list_a = load_list("list_a", offs, J)
         q2_raw = [load_query_half("q2_raw%d" % h, query2, h) for h in range(2)]
+        list_a = load_list("list_a", offs, J)
+        list_put = load_list("list_put", offs3, I)
         notes_w = keep.tile([P, U], I32, name="notes_w", align_bytes=64)
         nc.sync.dma_start(notes_w[:], notes_words[0].rearrange("p n t -> p (n t)").bitcast(I32))
-        list_put = load_list("list_put", offs3, I)
         load_plane(nc.sync, notes_plane, notes_scales)
         list_b = load_list("list_b", offs2, J)
         list_cc = load_list("list_cc", offs4, I)
@@ -96,7 +98,7 @@ def tile_attend_joinedput_twoq_mixed_kernel(tc, query, query2, keys_words, keys_
         a = [keep.tile([P, T], F32, name="a%d" % t) for t in range(PACK)]
         b = [keep.tile([P, U], F32, name="b%d" % t) for t in range(PACK)]
         w = [keep.tile([P, I], F32, name="w%d" % t) for t in range(PACK)]
-        g = [keep.tile([P, I], F32, name="g%d" % t)[:] for t in (0, 1, 3)]
+        g = [keep.tile([P, I], F32, name="g%d" % t) for t in range(PACK)]
         cc = [keep.tile([P, T], F32, name="cc%d" % t) for t in range(PACK)]
         a_banks = {}
 
@@ -143,24 +145,24 @@ def tile_attend_joinedput_twoq_mixed_kernel(tc, query, query2, keys_words, keys_
         def gpsimd_cast(dst, src):
             nc.gpsimd.tensor_scalar(dst, src, 1.0, 0.0, ALU.mult, ALU.add)
 
-        deal(nc.vector.tensor_copy, q_dealt, q_raw, 0, 0, 4)
+        deal(nc.vector.tensor_copy, q_dealt, q_raw, 0, 0, 2)
+        deal(nc.scalar.copy, q_dealt, q_raw, 0, 2, 4)
+        for quad in range(4):
+            rows = slice(32 * quad, 32 * quad + 4)
+            nc.vector.tensor_copy(keys_plane[rows, :].bitcast(I32), keys_rows[rows, :].bitcast(I32))
         deal(nc.vector.tensor_copy, q_dealt, q_raw, 1, 0, 1)
-        deal(nc.scalar.copy, q_dealt, q_raw, 1, 3, 4)
-        deal(nc.vector.tensor_copy, q_dealt, q_raw, 1, 1, 3)
         quantize_rows(q_codes, q_plane, q_dealt, 0, 1)
+        deal(nc.vector.tensor_copy, q_dealt, q_raw, 1, 1, 3)
+        deal(nc.scalar.copy, q_dealt, q_raw, 1, 3, 4)
         quantize_rows(q_codes, q_plane, q_dealt, 1, 4)
         part_a(0, nc.vector.tensor_copy, nc.vector.tensor_copy)
-        deal(nc.vector.tensor_copy, q2_dealt, q2_raw, 0, 0, 4)
-        deal(gpsimd_cast, q2_dealt, q2_raw, 1, 0, 1)
-        deal(gpsimd_cast, q2_dealt, q2_raw, 1, 1, 4)
-        quantize_rows(q2_codes, q2_plane, q2_dealt, 0, 1)
-        quantize_rows(q2_codes, q2_plane, q2_dealt, 1, 4)
+        deal(gpsimd_cast, q2_dealt, q2_raw, 0, 0, 4)
+        deal(gpsimd_cast, q2_dealt, q2_raw, 1, 0, 4)
+        quantize_rows(q2_codes, q2_plane, q2_dealt, 0, 4)
         part_a(1, nc.scalar.copy, scalar_gather)
-        part_b(0)
-        take_off(0)
         part_a(2, nc.scalar.copy, scalar_gather)
         last = PACK - 1
-        for t in range(1, last):
+        for t in range(last):
             part_b(t)
             take_off(t)
         part_a(last, nc.scalar.copy, scalar_gather)
@@ -178,14 +180,11 @@ def tile_attend_joinedput_twoq_mixed_kernel(tc, query, query2, keys_words, keys_
             nc.scalar.activation(pair_tile[:, t // 2, slots, t % 2], g[t][:, slots], COPY, scale=factors[:, t:t + 1])
 
         left = keep.tile([P, 3, I], F32, name="b%d" % last)
-        g.insert(2, left[:, 2, :])
-        for t in range(2):
+        for t in range(last):
             scalar_gather(left[:, t, :], cc[t][:].indirect(list_cc[:]))
-        for t in range(2):
-            nc.vector.tensor_tensor(g[t], left[:, t, :], w[t][:], ALU.add)
+        for t in range(last):
+            nc.vector.tensor_tensor(g[t][:], left[:, t, :], w[t][:], ALU.add)
             scale(t, slice(0, I))
-        nc.vector.tensor_tensor(g[2], cc[2][:].indirect(list_cc[:]), w[2][:], ALU.add)
-        scale(2, slice(0, I))
         for half in range(2):
             slots = slice(half * J, (half + 1) * J)
             nc.vector.tensor_tensor(g[last][:, slots], cc[last][:].indirect(list_cc[:, 16 * half:16 * (half + 1)]), w[last][:, slots], ALU.add)

@@ -98,25 +98,25 @@ def tile_attend_joinedput_twoq_mixed_kernel(tc, query, query2, keys_words, keys_
         a = [keep.tile([P, T], F32, name="a%d" % t) for t in range(PACK)]
         b = [keep.tile([P, U], F32, name="b%d" % t) for t in range(PACK)]
         w = [keep.tile([P, I], F32, name="w%d" % t) for t in range(PACK)]
-        g = [keep.tile([P, I], F32, name="g%d" % t) for t in range(PACK)]
+        g = [keep.tile([P, I], F32, name="g%d" % t)[:] for t in range(PACK - 1)]
         cc = [keep.tile([P, T], F32, name="cc%d" % t) for t in range(PACK)]
         a_banks = {}
 
-        def scores(t, codes, plane, words, pool_plane):
+        def scores(t, codes, plane, words, pool_plane, cuts):
             banks = []
-            for n in range(2):
-                bank = score_banks.tile([P, BANK], F32, name="score_bank")
+            for c0, c1 in zip(cuts, cuts[1:]):
+                bank = score_banks.tile([P, c1 - c0], F32, name="score_bank")
                 nc.tensor.matmul_mx(out=bank[:], lhsT=codes[:, t * P:(t + 1) * P].bitcast(FP8X4),
-                                    lhsT_scale=plane[:, t * P:(t + 1) * P], rhs=words(n),
-                                    rhs_scale=pool_plane[:, n * BANK:(n + 1) * BANK], start=True, stop=True)
+                                    lhsT_scale=plane[:, t * P:(t + 1) * P], rhs=words(c0, c1),
+                                    rhs_scale=pool_plane[:, c0:c1], start=True, stop=True)
                 banks.append(bank)
             return banks
 
-        def keys_cols(n):
-            return keys_w[:, 2 * n * BANK:2 * (n + 1) * BANK].bitcast(FP4X4)
+        def keys_cols(c0, c1):
+            return keys_w[:, 2 * c0:2 * c1].bitcast(FP4X4)
 
-        def notes_cols(n):
-            return notes_w[:, n * BANK:(n + 1) * BANK].bitcast(FP8X4)
+        def notes_cols(c0, c1):
+            return notes_w[:, c0:c1].bitcast(FP8X4)
 
         def scalar_gather(dst, src):
             nc.scalar.activation(dst, src, COPY)
@@ -124,16 +124,17 @@ def tile_attend_joinedput_twoq_mixed_kernel(tc, query, query2, keys_words, keys_
         def put(t, part):
             nc.vector.tensor_copy(placed[t % 3][:].indirect(list_put[:, 16 * part:16 * (part + 1)]), w[t][:, part * J:(part + 1) * J])
 
-        def part_a(t, second_copy, gather):
-            banks = scores(t, q_codes, q_plane, keys_cols, keys_plane)
+        def part_a(t, second_copy, gather, cuts=(0, BANK, T)):
+            banks = scores(t, q_codes, q_plane, keys_cols, keys_plane, cuts)
             a_banks[t] = banks
             nc.scalar.copy(a[t][:, :BANK], banks[0][:])
-            second_copy(a[t][:, BANK:], banks[1][:])
+            for c0, c1, bank in zip(cuts[1:], cuts[2:], banks[1:]):
+                second_copy(a[t][:, c0:c1], bank[:])
             gather(w[t][:, :J], a[t][:].indirect(list_a[:]))
             put(t, 0)
 
         def part_b(t):
-            banks = scores(t, q2_codes, q2_plane, notes_cols, notes_plane)
+            banks = scores(t, q2_codes, q2_plane, notes_cols, notes_plane, (0, BANK, U))
             nc.scalar.copy(b[t][:, :BANK], banks[0][:])
             nc.scalar.copy(b[t][:, BANK:], banks[1][:])
             scalar_gather(w[t][:, J:], b[t][:].indirect(list_b[:]))
@@ -145,8 +146,7 @@ def tile_attend_joinedput_twoq_mixed_kernel(tc, query, query2, keys_words, keys_
         def gpsimd_cast(dst, src):
             nc.gpsimd.tensor_scalar(dst, src, 1.0, 0.0, ALU.mult, ALU.add)
 
-        deal(nc.vector.tensor_copy, q_dealt, q_raw, 0, 0, 2)
-        deal(nc.scalar.copy, q_dealt, q_raw, 0, 2, 4)
+        deal(nc.scalar.copy, q_dealt, q_raw, 0, 0, 4)
         for quad in range(4):
             rows = slice(32 * quad, 32 * quad + 4)
             nc.vector.tensor_copy(keys_plane[rows, :].bitcast(I32), keys_rows[rows, :].bitcast(I32))
@@ -155,7 +155,7 @@ def tile_attend_joinedput_twoq_mixed_kernel(tc, query, query2, keys_words, keys_
         deal(nc.vector.tensor_copy, q_dealt, q_raw, 1, 1, 3)
         deal(nc.scalar.copy, q_dealt, q_raw, 1, 3, 4)
         quantize_rows(q_codes, q_plane, q_dealt, 1, 4)
-        part_a(0, nc.vector.tensor_copy, nc.vector.tensor_copy)
+        part_a(0, nc.vector.tensor_copy, nc.vector.tensor_copy, (0, BANK, BANK + BANK // 2, T))
         deal(gpsimd_cast, q2_dealt, q2_raw, 0, 0, 4)
         deal(gpsimd_cast, q2_dealt, q2_raw, 1, 0, 4)
         quantize_rows(q2_codes, q2_plane, q2_dealt, 0, 4)
@@ -180,23 +180,27 @@ def tile_attend_joinedput_twoq_mixed_kernel(tc, query, query2, keys_words, keys_
             nc.scalar.activation(pair_tile[:, t // 2, slots, t % 2], g[t][:, slots], COPY, scale=factors[:, t:t + 1])
 
         left = keep.tile([P, 3, I], F32, name="b%d" % last)
+        g.append(left[:, last - 1, :])
         for t in range(last):
             scalar_gather(left[:, t, :], cc[t][:].indirect(list_cc[:]))
         for t in range(last):
-            nc.vector.tensor_tensor(g[t][:], left[:, t, :], w[t][:], ALU.add)
+            adder = nc.gpsimd if t == 0 else nc.vector
+            adder.tensor_tensor(g[t], left[:, t, :], w[t][:], ALU.add)
             scale(t, slice(0, I))
         for half in range(2):
             slots = slice(half * J, (half + 1) * J)
             nc.vector.tensor_tensor(g[last][:, slots], cc[last][:].indirect(list_cc[:, 16 * half:16 * (half + 1)]), w[last][:, slots], ALU.add)
             scale(last, slots)
-        pair_words = pair_tile[:].rearrange("p k i r -> p k (i r)").bitcast(I32)
-        gw_words = gw[:].rearrange("p i t -> p (i t)").bitcast(I32).rearrange("p (i k) -> p i k", k=2)
+        pair_words = pair_tile[:].rearrange("p k i r -> p k (i r)")
+        gw_words = gw[:].rearrange("p i t -> p (i t)")
         for half in range(2):
             slots = slice(half * J, (half + 1) * J)
-            nc.vector.tensor_copy(gw_words[:, slots, :], pair_words[:, :, slots].rearrange("p k i -> p i k"))
+            weave, word = nc.vector.tensor_copy, I32
+            weave(gw_words.bitcast(word).rearrange("p (i k) -> p i k", k=2)[:, slots, :],
+                  pair_words.bitcast(word)[:, :, slots].rearrange("p k i -> p i k"))
             nc.vector.quantize_mx(out=gw_codes[:, slots].bitcast(FP8X4), scales=gw_plane[:, slots],
                                   in_=gw[:, slots, :].rearrange("p i t -> p (i t)"))
-            for e, copy in enumerate((nc.scalar.copy, nc.vector.tensor_copy)):
+            for e, copy in enumerate((nc.scalar.copy, nc.vector.tensor_copy if half else nc.scalar.copy)):
                 chans = slice(e * P, (e + 1) * P)
                 bank = out_banks.tile([P, J], F32, name="out_bank")
                 nc.tensor.matmul_mx(out=bank[:], lhsT=mix_w[:, chans].bitcast(FP8X4), lhsT_scale=mix_plane[:, chans],

from contextlib import ExitStack

import concourse.mybir as mybir

D, T, U, I, J, Q, E = 512, 1024, 1024, 512, 256, 512, 256
FLOPS = 2 * D * Q * T + 2 * D * Q * U + 2 * Q * E * I

F32 = mybir.dt.float32
BF16 = mybir.dt.bfloat16
I32 = mybir.dt.int32
U32 = mybir.dt.uint32
U16 = mybir.dt.uint16
U8 = mybir.dt.uint8
FP8X4 = mybir.dt.float8_e4m3fn_x4
FP4X4 = mybir.dt.float4_e2m1fn_x4
ALU = mybir.AluOpType
COPY = mybir.ActivationFunctionType.Copy

P = 128
PACK = 4
BANK = 512


def tile_attend_joinedput_twoq_mixed_kernel(tc, query, query2, keys_words, keys_scales, notes_words, notes_scales,
                                             rowf, mix_words, mix_scales, offs, offs2, offs3, offs4, out):
    nc = tc.nc
    with ExitStack() as ctx:
        keep = ctx.enter_context(tc.tile_pool(name="keep", bufs=1))
        score_banks = ctx.enter_context(tc.psum_pool(name="score_banks", bufs=4))
        out_banks = ctx.enter_context(tc.psum_pool(name="out_banks", bufs=4))

        def load_list(name, src, n):
            tile = keep.tile([P, n // 16], U16, name=name)
            nc.sync.dma_start(tile[:], src)
            return tile

        def zeroed_plane(name, width):
            tile = keep.tile([P, width], U8, name=name, align_bytes=64)
            nc.gpsimd.memset(tile[:].bitcast(I32), 0)
            return tile

        def load_plane(queue, tile, src):
            for quad in range(4):
                queue.dma_start(tile[32 * quad:32 * quad + 4, :].bitcast(I32), src[0, 4 * quad:4 * quad + 4, :].bitcast(I32))

        def load_query_half(name, src, half):
            tile = keep.tile([P, PACK, Q // 2], F32, name=name)
            nc.sync.dma_start(tile[:], src.rearrange("(p j) q -> p j q", j=PACK)[:, :, half * (Q // 2):(half + 1) * (Q // 2)])
            return tile

        keys_plane = zeroed_plane("keys_plane", T)
        notes_plane = zeroed_plane("notes_plane", U)
        mix_plane = zeroed_plane("mix_plane", E)

        q_raw = [load_query_half("q_raw0", query, 0)]
        keys_rows = keep.tile([P, T], U8, name="keys_rows", align_bytes=64)
        load_plane(nc.sync, keys_rows, keys_scales)
        q_raw.append(load_query_half("q_raw1", query, 1))
        keys_w = keep.tile([P, 2 * T], U8, name="keys_w", align_bytes=64)
        nc.sync.dma_start(keys_w[:].bitcast(I32), keys_words[0].bitcast(I32))
        q2_raw = [load_query_half("q2_raw%d" % h, query2, h) for h in range(2)]
        list_a = load_list("list_a", offs, J)
        list_put = load_list("list_put", offs3, I)
        notes_w = keep.tile([P, U], I32, name="notes_w", align_bytes=64)
        nc.sync.dma_start(notes_w[:], notes_words[0].rearrange("p n t -> p (n t)").bitcast(I32))
        load_plane(nc.sync, notes_plane, notes_scales)
        list_b = load_list("list_b", offs2, J)
        list_cc = load_list("list_cc", offs4, I)
        factors = keep.tile([P, PACK], F32, name="factors")
        nc.sync.dma_start(factors[:], rowf.rearrange("(p t) o -> p (t o)", t=PACK))
        mix_w = keep.tile([P, E], I32, name="mix_w", align_bytes=64)
        nc.sync.dma_start(mix_w[:], mix_words[0].rearrange("p n t -> p (n t)").bitcast(I32))
        load_plane(nc.sync, mix_plane, mix_scales)

        placed = [keep.tile([P, T], F32, name="placed%d" % k) for k in range(3)]
        for tile in placed:
            nc.vector.memset(tile[:], 0.0)

        def deal(copy, dealt, raw, half, t0, t1):
            src = raw[half][:].rearrange("p j (m t) -> p m t j", t=PACK)[:, :, t0:t1]
            dst = dealt[:].rearrange("p t m j -> p m t j")[:, 64 * half:64 * (half + 1), t0:t1]
            copy(dst, src)

        def quantize_rows(codes, plane, dealt, t0, t1):
            nc.vector.quantize_mx(
                out=codes[:, t0 * P:t1 * P].bitcast(FP8X4),
                scales=plane[:, t0 * P:t1 * P],
                in_=dealt[:, t0:t1].rearrange("p t m j -> p (t m j)"),
            )

        q_dealt = keep.tile([P, PACK, P, PACK], BF16, name="q_dealt", align_bytes=64)
        q_codes = keep.tile([P, Q], U32, name="q_codes", align_bytes=64)
        q_plane = keep.tile([P, Q], U8, name="q_plane", align_bytes=64)
        q2_dealt = keep.tile([P, PACK, P, PACK], BF16, name="q2_dealt", align_bytes=64)
        q2_codes = keep.tile([P, Q], U32, name="q2_codes", align_bytes=64)
        q2_plane = keep.tile([P, Q], U8, name="q2_plane", align_bytes=64)

        a = [keep.tile([P, T], F32, name="a%d" % t) for t in range(PACK)]
        b = [keep.tile([P, U], F32, name="b%d" % t) for t in range(PACK)]
        w = [keep.tile([P, I], F32, name="w%d" % t) for t in range(PACK)]
        g = [keep.tile([P, I], F32, name="g%d" % t)[:] for t in range(PACK - 1)]
        cc = [keep.tile([P, T], F32, name="cc%d" % t) for t in range(PACK)]
        a_banks = {}

        def scores(t, codes, plane, words, pool_plane, cuts):
            banks = []
            for c0, c1 in zip(cuts, cuts[1:]):
                bank = score_banks.tile([P, c1 - c0], F32, name="score_bank")
                nc.tensor.matmul_mx(out=bank[:], lhsT=codes[:, t * P:(t + 1) * P].bitcast(FP8X4),
                                    lhsT_scale=plane[:, t * P:(t + 1) * P], rhs=words(c0, c1),
                                    rhs_scale=pool_plane[:, c0:c1], start=True, stop=True)
                banks.append(bank)
            return banks

        def keys_cols(c0, c1):
            return keys_w[:, 2 * c0:2 * c1].bitcast(FP4X4)

        def notes_cols(c0, c1):
            return notes_w[:, c0:c1].bitcast(FP8X4)

        def scalar_gather(dst, src):
            nc.scalar.activation(dst, src, COPY)

        def put(t, part):
            nc.vector.tensor_copy(placed[t % 3][:].indirect(list_put[:, 16 * part:16 * (part + 1)]), w[t][:, part * J:(part + 1) * J])

        def part_a(t, second_copy, gather, cuts=(0, BANK, T)):
            banks = scores(t, q_codes, q_plane, keys_cols, keys_plane, cuts)
            a_banks[t] = banks
            nc.scalar.copy(a[t][:, :BANK], banks[0][:])
            for c0, c1, bank in zip(cuts[1:], cuts[2:], banks[1:]):
                second_copy(a[t][:, c0:c1], bank[:])
            gather(w[t][:, :J], a[t][:].indirect(list_a[:]))
            put(t, 0)

        def part_b(t):
            banks = scores(t, q2_codes, q2_plane, notes_cols, notes_plane, (0, BANK, U))
            nc.scalar.copy(b[t][:, :BANK], banks[0][:])
            nc.scalar.copy(b[t][:, BANK:], banks[1][:])
            scalar_gather(w[t][:, J:], b[t][:].indirect(list_b[:]))
            put(t, 1)

        def take_off(t):
            nc.gpsimd.tensor_tensor(cc[t][:], a[t][:], placed[t % 3][:], ALU.subtract)

        def gpsimd_cast(dst, src):
            nc.gpsimd.tensor_scalar(dst, src, 1.0, 0.0, ALU.mult, ALU.add)

        deal(nc.scalar.copy, q_dealt, q_raw, 0, 0, 4)
        for quad in range(4):
            rows = slice(32 * quad, 32 * quad + 4)
            nc.vector.tensor_copy(keys_plane[rows, :].bitcast(I32), keys_rows[rows, :].bitcast(I32))
        deal(nc.vector.tensor_copy, q_dealt, q_raw, 1, 0, 1)
        quantize_rows(q_codes, q_plane, q_dealt, 0, 1)
        deal(nc.vector.tensor_copy, q_dealt, q_raw, 1, 1, 3)
        deal(nc.scalar.copy, q_dealt, q_raw, 1, 3, 4)
        quantize_rows(q_codes, q_plane, q_dealt, 1, 4)
        part_a(0, nc.vector.tensor_copy, nc.vector.tensor_copy, (0, BANK, BANK + BANK // 2, T))
        deal(gpsimd_cast, q2_dealt, q2_raw, 0, 0, 4)
        deal(gpsimd_cast, q2_dealt, q2_raw, 1, 0, 4)
        quantize_rows(q2_codes, q2_plane, q2_dealt, 0, 4)
        part_a(1, nc.scalar.copy, scalar_gather)
        part_a(2, nc.scalar.copy, scalar_gather)
        last = PACK - 1
        for t in range(last):
            part_b(t)
            take_off(t)
        part_a(last, nc.scalar.copy, scalar_gather)
        part_b(last)
        for n in range(2):
            cols = slice(n * BANK, (n + 1) * BANK)
            nc.vector.tensor_tensor(cc[last][:, cols], a_banks[last][n][:], placed[last % 3][:, cols], ALU.subtract)

        pair_tile = keep.tile([P, 2, I, 2], BF16, name="pair_tile", align_bytes=64)
        gw = keep.tile([P, I, PACK], BF16, name="gw", align_bytes=64)
        gw_codes = keep.tile([P, I], U32, name="gw_codes", align_bytes=64)
        gw_plane = keep.tile([P, I], U8, name="gw_plane", align_bytes=64)

        def scale(t, slots):
            nc.scalar.activation(pair_tile[:, t // 2, slots, t % 2], g[t][:, slots], COPY, scale=factors[:, t:t + 1])

        left = keep.tile([P, 3, I], F32, name="b%d" % last)
        g.append(left[:, last - 1, :])
        for t in range(last):
            scalar_gather(left[:, t, :], cc[t][:].indirect(list_cc[:]))
        for t in range(last):
            adder = nc.gpsimd if t == 0 else nc.vector
            adder.tensor_tensor(g[t], left[:, t, :], w[t][:], ALU.add)
            scale(t, slice(0, I))
        for half in range(2):
            slots = slice(half * J, (half + 1) * J)
            nc.vector.tensor_tensor(g[last][:, slots], cc[last][:].indirect(list_cc[:, 16 * half:16 * (half + 1)]), w[last][:, slots], ALU.add)
            scale(last, slots)
        pair_words = pair_tile[:].rearrange("p k i r -> p k (i r)")
        gw_words = gw[:].rearrange("p i t -> p (i t)")
        for half in range(2):
            slots = slice(half * J, (half + 1) * J)
            weave, word = nc.vector.tensor_copy, I32
            weave(gw_words.bitcast(word).rearrange("p (i k) -> p i k", k=2)[:, slots, :],
                  pair_words.bitcast(word)[:, :, slots].rearrange("p k i -> p i k"))
            nc.vector.quantize_mx(out=gw_codes[:, slots].bitcast(FP8X4), scales=gw_plane[:, slots],
                                  in_=gw[:, slots, :].rearrange("p i t -> p (i t)"))
            for e, copy in enumerate((nc.scalar.copy, nc.vector.tensor_copy if half else nc.scalar.copy)):
                chans = slice(e * P, (e + 1) * P)
                bank = out_banks.tile([P, J], F32, name="out_bank")
                nc.tensor.matmul_mx(out=bank[:], lhsT=mix_w[:, chans].bitcast(FP8X4), lhsT_scale=mix_plane[:, chans],
                                    rhs=gw_codes[:, slots].bitcast(FP8X4), rhs_scale=gw_plane[:, slots], start=True, stop=True)
                staged = keep.tile([P, J], F32, name="staged%d_%d" % (half, e))
                copy(staged[:], bank[:])
                nc.sync.dma_start(out[chans, slots], staged[:])
